import numpy as np
CORES = [76,84,92,100,108,116,124]
N = 7
R, E = 8192, 2048
CAPP = 1024
def entries(a): return a.T.reshape(-1)
def pack(v, P): return np.ascontiguousarray(np.asarray(v, np.int32).reshape(-1, P).T)
def lists(rng, how):
    n = N * E; q = np.arange(n) // E
    P = rng.permutation(np.repeat(np.arange(N * N), CAPP))[:n]
    if how == "full":
        a = rng.integers(0, N); z = np.delete(np.arange(N), a); o = rng.permutation(N * N); o = o[(o // N != a) & (o % N != a) & (o // N != o % N)]
        C = np.concatenate([N * a + rng.permutation(z), [(N + 1) * a], N * rng.permutation(z) + a, o])[:n // CAPP]
        L = np.repeat(C, CAPP).reshape(N, E); s, t = 1 + 2 * rng.integers(0, CAPP // 8, 2); t += 2 * (CAPP // 8)
        L[0, :s], L[1, :s] = C[E // CAPP], C[0]; L[0, s:s + t], L[N - 1, E - t:] = C[-1], C[0]
        L = L[rng.permutation(N)]; L[0] = L[0].reshape(16, -1).T.reshape(-1)
        for r in range(1, N, 2): L[r] = rng.permutation(L[r])
        P = L.reshape(-1)
    if how == "same":
        o = np.arange(N * N); o = rng.permutation(np.repeat(o[o % (N + 1) != 0], CAPP))[:n - N * CAPP].reshape(N, E - CAPP)
        P = np.stack([rng.permutation(np.append(o[r], np.full(CAPP, (N + 1) * r))) for r in range(N)]).reshape(-1)
    if how == "cross":
        d = np.stack([rng.permutation(1 + np.arange(E) % (N - 1)) for r in range(N)]).reshape(-1); a = 1 + rng.integers(0, N - 2, N); a += a >= N - np.arange(N)
        P = (q + a[d]) % N * N + (q + a[d] + d) % N
    if how == "edge": k = rng.permutation(n); P = k % (N * N)
    h, g = P // N, P % N; u, v = rng.integers(0, R, n), rng.integers(0, R, n)
    if how == "alike": u, v = rng.integers(0, R, N * N)[P], rng.integers(0, R, N * N)[P]
    if how == "edge": u, v = (R - 1) * (k // (N * N) % 2), (R - 1) * (k // (2 * N * N) % 2)
    if how == "full": u, v = (np.stack([rng.permutation(R)[np.arange(E) % R] for r in range(N)]).reshape(-1) for _ in range(2))
    if how == "same": v = u
    return {"pi": np.stack([pack(w, 16) for w in (R * h + u).reshape(N, E)]), "pj": np.stack([pack(w, 16) for w in (R * g + v).reshape(N, E)])}
def setup_inputs(rng):
    return dict({"ta": rng.standard_normal((N, 128, R), dtype=np.float32), "tb": rng.standard_normal((N, 128, R), dtype=np.float32)}, **lists(rng, "uniform"))
def setup_inputs_alike(rng):
    d = setup_inputs(rng); d.update(lists(rng, "alike"))
    for k in ("ta", "tb"): d[k] = (d[k].astype(np.float32) * 1024.0).astype(d[k].dtype)
    return d
def setup_inputs_cross(rng):
    d = setup_inputs(rng); d.update(lists(rng, "cross"))
    for k in ("ta", "tb"): d[k] = (d[k].astype(np.float32) * (1 / 1024.0)).astype(d[k].dtype)
    return d
def setup_inputs_edge(rng):
    d = setup_inputs(rng); d.update(lists(rng, "edge"))
    return d
def setup_inputs_full(rng):
    d = setup_inputs(rng); d.update(lists(rng, "full"))
    return d
def setup_inputs_same(rng):
    d = setup_inputs(rng); d.update(lists(rng, "same"))
    return d
def check_inputs(x):
    bad = []
    if x["pi"].min() < 0 or x["pi"].max() >= N * R: bad.append("pi out of range")
    if x["pj"].min() < 0 or x["pj"].max() >= N * R: bad.append("pj out of range")
    if not bad and int(np.bincount((x["pi"] // R * N + x["pj"] // R).reshape(-1), minlength=N * N).max()) > CAPP: bad.append("more than CAPP pairs with i in one rank's part of TA and j in one rank's part of TB")
    return bad
def reference(ta, tb, pi, pj):
    A, B = np.concatenate(list(ta), axis=1).astype(np.float64), np.concatenate(list(tb), axis=1).astype(np.float64)
    y = []
    for r in range(N):
        i, j = entries(pi[r]), entries(pj[r])
        y.append((A[:, i] * B[:, j]).sum(axis=0))
    return {"y": np.stack(y).reshape(N, -1, 16).transpose(0, 2, 1).astype(np.float32)}

from concourse.bass import DstId, RemoteDMATransfer
from concourse.mybir import AluOpType, ActivationFunctionType

N = 7
R = 8192
C1, C2 = 592, 512
LW = 80
BATCH = [(0, 4), (4, 6), (6, 7)]

_F, _H, _I, _U, _B = "float32", "float16", "int32", "uint16", "bfloat16"
_SBUF = [
    ("TAs", R, _F), ("TBs", R, _F), ("X", 128, _I), ("Y", 64, _I), ("LR", N * LW, _B), ("D", 2048, _B), ("win", 9216, _B),
    ("F", 112, _B), ("M", 784, _B), ("VM", 784, _H), ("S", 784, _F), ("P16", 128, _U), ("OFJ", 448, _U), ("OFI", 448, _U),
    ("MS1", N * C1, _F), ("MS2", N * C2, _F), ("R1", N * C1, _F), ("R2", N * C2, _F), ("PR", N * 1024, _F), ("SW", 3136, _F),
    ("IOD", 128, _F), ("IPI", 1, _I), ("IXM", 144, _F), ("IN", 448, _F), ("IRS", 448, _F), ("IPC", 128, _F), ("NC", 16, _F),
    ("IO16", 16, _F), ("IG", 128, _F), ("PIA", 4, _I), ("PC4", 4, _F), ("SEL", 2, _F), ("BJ", 144, _B), ("BI", 144, _B),
    ("RB", 144, _F), ("ID", 128, _F), ("IDF", 128, _H), ("TRI", 128, _B), ("ONES", 128, _B), ("IDH", N * 128, _B),
    ("IDW", N * 128, _B), ("NT", 448, _H), ("RST", 448, _F), ("PC", 128, _F), ("BDC", 8, _F), ("DT", 16, _F), ("G8", 128, _B),
    ("ACC", N * 16, _F), ("VI", 80, _I), ("AF", 48, _F), ("QB", 16, _B), ("Q8", 256, _B), ("LC", 128, _F), ("O16", 16, _U),
    ("FP", 512, _F),
]
SCRATCH = {n: ("sbuf", [128, w], d) for n, w, d in _SBUF}
SCRATCH.update({"b%d" % k: ("psum", [128, 512], _F) for k in range(8)})

SEMAPHORES = ["v", "t", "s", "gi", "snt", "ldy", "ldx", "ldtb", "ldta", "dl", "go", "go2", "ldq", "yo"]
SEMAPHORES += ["lst%d" % r for r in range(N)] + ["h%d_%d" % (h, r) for h in (1, 2) for r in range(N)]
SEMAPHORES += ["sc%d_%d" % (r, i) for r in range(N) for i in range(len(BATCH))]


def make_plan(T, topo):
    cores = list(T.cores)
    chip = [topo.chip(c) for c in cores]
    allc = range(topo.CHIPS * topo.CORES_PER_CHIP)
    near, far, helper, same, slot = [], [], [], [], {}
    for r in range(N):
        grp = [q for q in range(N) if q == r or topo.same_plane(chip[r], chip[q])]
        oth = [q for q in range(N) if q not in grp]
        i = grp.index(r)
        ys = [grp[(i + 1 + k) % len(grp)] for k in range(len(grp) - 1)]
        xs = [oth[(i + k) % len(oth)] for k in range(len(oth))]
        same.append(ys)
        near.append(xs[:3])
        far.append(ys + xs[3:])
        for lane in (near[r], far[r]):
            for k, q in enumerate(lane):
                slot[(r, q)] = k + (0.6 if q in oth else 0.0)
        own = [c for c in allc if topo.chip(c) == chip[r] and c != cores[r] and all(topo.may_write(c, cores[q]) for q in oth)]
        here = [c for c in own if topo.die(c) == topo.die(cores[r])]
        there = [c for c in own if topo.die(c) != topo.die(cores[r])]
        first = ([q for q in xs if topo.mates(chip[r], chip[q])] or xs)[0]
        hp = {first: here[0]}
        for k, q in enumerate([q for q in xs if q != first]):
            hp[q] = there[k % len(there)]
        helper.append(hp)
    order = [[a] + sorted([b for b in range(N) if b != a], key=lambda b: (slot[(b, a)], b)) for a in range(N)]
    return {"cores": cores, "same": same, "near": near, "far": far, "helper": helper, "order": order}


def rank_program(g, core, T, topo):
    rank = T.rank_of(core)
    P = make_plan(T, topo)
    cores = P["cores"]
    sent = [0]

    def bits(m):
        return bin(m).count("1")

    def did(c):
        a = topo.addr(c)
        return DstId(rid=a[0], pnc=a[1])

    def transfer(mask, dsts, sem, src, dst):
        sent[0] += bits(mask)
        return RemoteDMATransfer(dst_ids=[did(c) for c in dsts], dma_engine_mask=mask, remote_sem=T.sem[sem],
                                 srcs=[src], dsts=[dst] * len(dsts), alu_op=0)

    def send(*tr):
        g.remote_dma_fused(list(tr), local_sem=T.sem.snt)

    def lists(r):
        return T.LR[:, r * LW:(r + 1) * LW]

    def half(buf1, buf2, h, r):
        return buf1[:, r * C1:(r + 1) * C1] if h == 1 else buf2[:, r * C2:(r + 1) * C2]

    def scores(a, i):
        lo, hi = BATCH[i]
        return T.SW[:, (7 * a + lo) * 64:(7 * a + hi) * 64]

    if rank is None:
        for r in range(N):
            hp = P["helper"][r]
            mine = [q for q in P["near"][r] + P["far"][r] if q in hp and hp[q] == core]
            if not mine:
                continue
            dst = [cores[q] for q in mine]
            mask = topo.mask(core, dst[0])
            eng = bits(mask)
            g.wait_ge(T.sem["lst%d" % r], eng)
            send(transfer(mask, dst, "lst%d" % r, lists(r), lists(r)))
            for q in mine:
                for h in (1, 2):
                    g.wait_ge(T.sem["h%d_%d" % (h, q)], eng)
                    send(transfer(mask, [cores[q]], "h%d_%d" % (h, r), half(T.R1, T.R2, h, q), half(T.R1, T.R2, h, r)))
            for i in range(len(BATCH)):
                g.wait_ge(T.sem["sc%d_%d" % (r, i)], eng)
                send(transfer(mask, dst, "sc%d_%d" % (r, i), scores(r, i), scores(r, i)))
            g.wait_ge(T.sem.snt, sent[0])
        return

    A = AluOpType
    COPY = ActivationFunctionType.Copy
    V, E, SC, SY = g.vector, g.tensor, g.scalar, g.sync
    queues = {"v": V, "t": E, "s": SC, "y": SY, "g": g}
    cnt = {"v": 0, "t": 0, "s": 0, "gi": 0}
    seen = {}

    def wait(q, sem, val):
        if val and seen.get((q, sem), 0) < val:
            queues[q].wait_ge(T.sem[sem], val)
            seen[(q, sem)] = val

    def done(eng_name, inst):
        inst.then_inc(T.sem[eng_name], 1)
        cnt[eng_name] += 1
        return cnt[eng_name]

    def v(inst):
        return done("v", inst)

    def t(inst):
        return done("t", inst)

    def s(inst):
        return done("s", inst)

    def iota(out, pattern, base, cm):
        return done("gi", g.iota(out[:], pattern, base, cm, allow_small_or_imprecise_dtypes=True))

    def ts(out, in0, s1, s2, op0, op1=None):
        if op1 is None:
            return v(V.tensor_scalar(out, in0, s1, None, op0))
        return v(V.tensor_scalar(out, in0, s1, s2, op0, op1))

    me = rank
    hp = P["helper"][me]
    helpers = sorted(set(hp.values()))
    same = P["same"][me]
    cross = [q for q in range(N) if q != me and q not in same]
    low = topo.mask(core, cores[same[0]])
    high = topo.mask(core, helpers[0]) & ~low
    eng = bits(low)

    SY.dma_start(T.Y[:, 0:16], T.pi[:]).then_inc(T.sem.ldy, 16)
    SC.dma_start(T.Y[:, 16:32], T.pj[:]).then_inc(T.sem.ldy, 16)
    SY.dma_start(T.X[0:32, 0:64], T.pi[:]).then_inc(T.sem.ldx, 16)
    SC.dma_start(T.X[32:64, 0:64], T.pj[:]).then_inc(T.sem.ldx, 16)
    SY.dma_start(T.X[64:96, 0:64], T.pi[:]).then_inc(T.sem.ldx, 16)
    SC.dma_start(T.X[96:128, 0:64], T.pj[:]).then_inc(T.sem.ldx, 16)
    SY.dma_start(T.TBs[:, 0:1024], T.tb[:, 0:1024]).then_inc(T.sem.ldtb, 16)

    done("gi", g.iota(T.IPI[:], [[1, 1]], 0, 1))
    g_od = iota(T.IOD, [[-1, 128]], 0, 1)
    iota(T.IXM, [[0, 9], [1, 16]], 0, 0)
    g_pc = iota(T.IPC, [[16, 128]], 7168, 0)

    v_d = v(V.memset(T.D[:], 0.0))
    v(V.memset(T.ONES[:], 1.0))
    v(V.memset(T.win[:, 0:3072], 0.0))
    wait("v", "ldy", 32)
    ts(T.Y[:, 32:48], T.Y[:, 0:16], 13, None, A.arith_shift_right)
    k1 = ts(T.Y[:, 48:64], T.Y[:, 16:32], 10, 56, A.arith_shift_right, A.bitwise_and)
    wait("v", "ldx", 64)
    ts(T.X[0:64, 64:128], T.X[0:64, 0:64], 8128, None, A.bitwise_and)
    k2 = ts(T.X[64:128, 64:128], T.X[64:128, 0:64], 63, None, A.bitwise_and)
    wait("v", "v", k1)
    v(V.tensor_tensor(T.LR[:, me * LW:me * LW + 16], T.Y[:, 32:48], T.Y[:, 48:64], A.add))
    wait("v", "v", k2)
    v_list = v(V.tensor_copy(T.LR[:, me * LW + 16:(me + 1) * LW], T.X[:, 64:128]))

    wait("g", "v", v_list)
    send(transfer(high, helpers, "lst%d" % me, lists(me), lists(me)))
    send(transfer(low, [cores[q] for q in same], "lst%d" % me, lists(me), lists(me)))
    g.sem_inc(T.sem.go, 1)
    wait("y", "go", 1)
    SY.dma_start(T.TBs[:, 1024:5120], T.tb[:, 1024:5120]).then_inc(T.sem.ldtb, 16)

    iota(T.IN, [[0, 28], [1, 16]], 0, 16)
    g_rs = iota(T.IRS, [[0, 4], [1, 112]], 0, 0)
    iota(T.NC, [[1, 16]], 0, 16)
    iota(T.IO16, [[1, 16]], 0, 0)
    g_end = iota(T.IG, [[1, 8], [0, 16]], 0, 0)

    wait("v", "gi", g_od)
    v_id = ts(T.ID[:], T.IOD[:], 0.0, None, A.is_equal)
    ts(T.IDF[:], T.IOD[:], 0.0, None, A.is_equal)
    ts(T.TRI[:], T.IOD[:], 0.0, None, A.is_ge)
    ts(T.PIA[:, 0:1], T.IPI[:], 15, None, A.bitwise_and)
    ts(T.PIA[:, 1:2], T.IPI[:], 4, None, A.arith_shift_right)
    ts(T.PIA[:, 2:3], T.IPI[:], 13, None, A.bitwise_and)
    k = v(V.tensor_copy(T.PIA[:, 3:4], T.IPI[:]))
    wait("v", "v", k)
    k = v(V.tensor_copy(T.PC4[:], T.PIA[:]))
    wait("v", "v", k)
    wait("v", "gi", g_pc)
    ts(T.SEL[:, 0:1], T.PC4[:, 2:3], 1.0, None, A.is_equal)
    ts(T.SEL[:, 1:2], T.PC4[:, 2:3], 0.0, None, A.is_equal)
    k = ts(T.PC[:], T.IPC[:], T.PC4[:, 0:1], None, A.add)
    wait("v", "v", k)
    v_pc = v(V.tensor_copy(T.P16[:], T.PC[:]))
    ts(T.BJ[:], T.IXM[:], 0.0, T.SEL[:, 0:1], A.is_equal, A.mult)
    ts(T.BI[:], T.IXM[:], 0.0, T.SEL[:, 1:2], A.is_equal, A.mult)
    ts(T.RB[:], T.IXM[:], 0.0, None, A.is_equal)
    wait("v", "gi", g_rs)
    ts(T.RST[:], T.IRS[:], 0.0, None, A.not_equal)
    v_nt = v(V.tensor_copy(T.NT[:], T.IN[:]))
    v(V.memset(T.win[:, 3072:7168], 0.0))

    wait("s", "v", v_id)
    pos = [P["order"][h].index(me) for h in range(N)]
    for h in range(N):
        s(SC.activation(T.IDH[:, h * 128:(h + 1) * 128], T.ID[:], COPY, scale=float(-1024 * (7 - h))))
        s_c = s(SC.activation(T.IDW[:, h * 128:(h + 1) * 128], T.ID[:], COPY, scale=float(1024 * (7 * h + pos[h]))))

    wait("t", "v", v_nt)
    E.matmul(T.b2[:, 0:448], T.IDF[:], T.NT[:], True, False)
    E.matmul(T.b3[:, 0:336], T.IDF[:], T.NT[:, 0:336], True, False)
    E.matmul(T.b6[0:112, 0:128], T.ID[:, 0:112], T.PC[:], True, False)

    for r in [me] + same + cross:
        if r == me:
            wait("s", "v", v_list)
            wait("v", "v", v_list)
        else:
            wait("v", "lst%d" % r, eng)
            wait("s", "lst%d" % r, eng)
        v_f = v(V.tensor_copy(T.F[:, 16 * r:16 * r + 16], T.LR[:, r * LW:r * LW + 16]))
        SC.dma_start(T.D[16 * r:16 * r + 4, :], T.LR[:, r * LW + 16:(r + 1) * LW]).then_inc(T.sem.dl, 16)
    SC.sem_inc(T.sem.go2, 1)
    wait("y", "go2", 1)
    SY.dma_start(T.TBs[:, 5120:8192], T.tb[:, 5120:8192]).then_inc(T.sem.ldtb, 16)
    SY.dma_start(T.TAs[:, 0:4096], T.ta[:, 0:4096]).then_inc(T.sem.ldta, 16)
    SY.dma_start(T.TAs[:, 4096:8192], T.ta[:, 4096:8192]).then_inc(T.sem.ldta, 16)

    parts = [(0, 4), (4, 7)]
    wait("v", "v", v_f)
    v_m = []
    for lo, hi in parts:
        for h in range(lo, hi):
            k = ts(T.M[:, h * 112:(h + 1) * 112], T.F[:], float(8 * me + h), None, A.is_equal)
        v_m.append(k)
    t_tl = []
    for i, (lo, hi) in enumerate(parts):
        w = (hi - lo) * 112
        wait("t", "v", v_m[i])
        a = t(E.matmul(T["b%d" % i][:, 0:w], T.ONES[:], T.M[:, lo * 112:hi * 112], True, True))
        b = t(E.matmul(T["b%d" % (2 + i)][:, 0:w], T.TRI[:], T.M[:, lo * 112:hi * 112], False, True))
        t_tl.append((a, b))
    wait("t", "s", s_c)
    for h in range(N):
        E.matmul(T.b6[0:112, 0:128], T.M[:, h * 112:(h + 1) * 112], T.IDH[:, h * 128:(h + 1) * 128], False, False)
    for h in range(N):
        E.matmul(T.b7[:, 0:112], T.IDW[:, h * 128:(h + 1) * 128], T.M[:, h * 112:(h + 1) * 112], h == 0, False)
    v_vm = [0, 0]
    ks = []
    for i, (lo, hi) in enumerate(parts):
        w = (hi - lo) * 112
        wait("v", "t", t_tl[i][0])
        ks.append(v(V.tensor_tensor_scan(T.S[:, lo * 112:hi * 112], T.RST[:, 0:w], T["b%d" % i][:, 0:w], 0.0, A.mult, A.add)))
    for i, (lo, hi) in enumerate(parts):
        w = (hi - lo) * 112
        wait("v", "t", t_tl[i][1])
        wait("v", "v", ks[i])
        k = v(V.tensor_tensor(T["b%d" % (4 + i)][:, 0:w], T.S[:, lo * 112:hi * 112], T["b%d" % (2 + i)][:, 0:w], A.subtract))
        wait("v", "v", k)
        v_vm[i] = v(V.tensor_tensor(T.VM[:, lo * 112:hi * 112], T["b%d" % (4 + i)][:, 0:w], T.M[:, lo * 112:hi * 112], A.mult))
    for i, (lo, hi) in enumerate(parts):
        wait("t", "v", v_vm[i])
        for h in range(lo, hi):
            mm = E.matmul(T.b6[0:112, 0:128], T.VM[:, h * 112:(h + 1) * 112], T.IDF[:], False, h == N - 1)
    t_idx = t(mm)
    for h in range(N):
        mm = E.matmul(T.b7[:, 0:112], T.IDF[:], T.VM[:, h * 112:(h + 1) * 112], False, h == N - 1)
    t_w = t(mm)
    wait("v", "t", t_idx)
    wait("v", "v", v_pc)
    k = v(V.tensor_copy(T.P16[0:112, :], T.b6[0:112, 0:128]))
    wait("v", "v", k)
    wait("v", "dl", 16 * N)
    v_sc = v(V.tensor_copy(T.win[:, 0:9216].indirect(T.P16[:, 0:128]), T.D[:]))

    dests = []
    for x, y in zip(P["near"][me], P["far"][me]):
        dests += [x, y]
    dests.append(me)
    ready, vj, si = {}, {}, {}
    for n, a in enumerate(dests):
        bj, bi = T["b%d" % (n % 2)], T["b%d" % (2 + n % 2)]
        wait("t", "v", v_sc if n < 2 else vj[n - 2])
        for q in range(16):
            o = a * 1024 + 64 * q
            mm = E.matmul(bj[:, 0:64], T.BJ[:, 16 - q:144 - q], T.win[:, o:o + 64], q == 0, q == 15)
        t_j = t(mm)
        if n >= 2:
            wait("t", "s", si[n - 2])
        for q in range(16):
            o = a * 1024 + 64 * q
            mm = E.matmul(bi[:, 0:64], T.BI[:, 16 - q:144 - q], T.win[:, o:o + 64], q == 0, q == 15)
        t_i = t(mm)
        wait("v", "t", t_j)
        vj[n] = v(V.tensor_copy(T.OFJ[:, a * 64:a * 64 + 64], bj[:, 0:64]))
        wait("v", "v", vj[n])
        wait("v", "ldtb", 48)
        v_h = v(V.tensor_copy(T.MS1[:, a * C1:a * C1 + 512], T.TBs[:, 0:R].indirect(T.OFJ[:, a * 64:a * 64 + 32])))
        wait("s", "t", t_w)
        s(SC.activation(T.MS1[:, a * C1 + 576:a * C1 + 592], T.b7[:, 16 * a:16 * a + 16], COPY))
        wait("s", "t", t_i)
        si[n] = s(SC.activation(T.MS1[:, a * C1 + 512:a * C1 + 576], bi[:, 0:64], COPY))
        wait("s", "v", vj[n])
        wait("s", "ldtb", 48)
        s_h = s(SC.activation(T.MS2[:, a * C2:(a + 1) * C2], T.TBs[:, 0:R].indirect(T.OFJ[:, a * 64 + 32:a * 64 + 64]), COPY))
        ready[a] = (v_h, si[n], s_h)

    def part(a, h, lane):
        if h == 1:
            wait("g", "v", ready[a][0])
            wait("g", "s", ready[a][1])
        else:
            wait("g", "s", ready[a][2])
        if a in hp:
            return transfer(lane, [hp[a]], "h%d_%d" % (h, a), half(T.MS1, T.MS2, h, a), half(T.R1, T.R2, h, a))
        return transfer(lane, [cores[a]], "h%d_%d" % (h, me), half(T.MS1, T.MS2, h, a), half(T.R1, T.R2, h, me))

    for n, (x, y) in enumerate(zip(P["near"][me], P["far"][me])):
        for h in (1, 2):
            px = part(x, h, high)
            if n == 0 and h == 1:
                send(px)
                send(part(y, h, low))
            else:
                send(px, part(y, h, low))

    wait("v", "gi", g_end)
    ts(T.BDC[:], T.IO16[:, 0:8], T.PC4[:, 1:2], None, A.is_equal)
    ts(T.DT[:], T.IO16[:], T.PC4[:, 0:1], None, A.is_equal)
    ts(T.G8[:], T.IG[:], T.PC4[:, 3:4], None, A.is_equal)
    wait("v", "ldta", 32)
    s_bank = {}
    for n, b in enumerate(P["order"][me]):
        last = n == N - 1
        if b == me:
            r1, r2, o1, o2 = T.MS1, T.MS2, me * C1, me * C2
            wait("v", "s", ready[me][2])
            wait("v", "v", ready[me][0])
        else:
            r1, r2, o1, o2 = T.R1, T.R2, b * C1, b * C2
            wait("v", "h1_%d" % b, eng)
        k = v(V.tensor_copy(T.OFI[:, b * 64:b * 64 + 64], r1[:, o1 + 512:o1 + 576]))
        wait("v", "v", k)
        bank = T["b%d" % (4 + n % 3)]
        v_p = [v(V.tensor_tensor(T.PR[:, b * 1024:b * 1024 + 512], T.TAs[:, 0:R].indirect(T.OFI[:, b * 64:b * 64 + 32]),
                                 r1[:, o1:o1 + 512], A.mult))]
        k = v(V.tensor_tensor(T.VI[:, 0:16] if last else T.ACC[:, 16 * n:16 * n + 16],
                              T.ACC[:, 16 * n - 16:16 * n] if n else T.NC[:], r1[:, o1 + 576:o1 + 592], A.add))
        if last:
            vi = T.VI[:, 0:16]
            wait("v", "v", k)
            k_q = ts(T.VI[:, 64:80], vi, 2, 15, A.arith_shift_right, A.bitwise_and)
            ts(T.VI[:, 16:32], vi, 4, 65472, A.arith_shift_right, A.bitwise_and)
            ts(T.VI[:, 32:48], vi, 6, 15, A.arith_shift_right, A.bitwise_and)
            k = ts(T.VI[:, 48:64], vi, 3, None, A.bitwise_and)
            wait("v", "v", k_q)
            k_q = v(V.tensor_copy(T.QB[:], T.VI[:, 64:80]))
            wait("v", "v", k)
            v(V.tensor_tensor(T.AF[:, 0:16], T.VI[:, 16:32], T.VI[:, 32:48], A.add))
            k = ts(T.AF[:, 16:32], T.VI[:, 48:64], 16.0, None, A.mult)
            wait("v", "v", k)
            k = v(V.tensor_tensor(T.AF[:, 32:48], T.AF[:, 0:16], T.AF[:, 16:32], A.add))
            wait("v", "v", k)
            for x in range(8):
                k_lc = ts(T.LC[:, 16 * x:16 * x + 16], T.AF[:, 32:48], T.BDC[:, x:x + 1], None, A.mult)
            wait("y", "v", k_q)
            SY.dma_start(T.Q8[0:8, :], T.QB[:]).then_inc(T.sem.ldq, 16)
        if b != me:
            wait("v", "h2_%d" % b, eng)
        step = 256 if last else 512
        for c in range(0, 512, step):
            j = 512 + c
            v_p.append(v(V.tensor_tensor(T.PR[:, b * 1024 + j:b * 1024 + j + step],
                                         T.TAs[:, 0:R].indirect(T.OFI[:, b * 64 + j // 16:b * 64 + (j + step) // 16]),
                                         r2[:, o2 + c:o2 + c + step], A.mult)))
        if n >= 3:
            wait("t", "s", s_bank[n - 3])
        j = 0
        for e, kv in zip([512] + list(range(512 + step, 1025, step)), v_p):
            wait("t", "v", kv)
            while j < e:
                q = j // 64
                mm = E.matmul(bank[:, 0:64], T.RB[:, 16 - q:144 - q], T.PR[:, b * 1024 + j:b * 1024 + j + 64], q == 0, q == 15)
                j += 64
        wait("s", "t", t(mm))
        o = (7 * me + n) * 64
        s_bank[n] = s(SC.activation(T.SW[:, o:o + 64], bank[:, 0:64], COPY))
        for i, (lo, hi) in enumerate(BATCH):
            if n == hi - 1:
                wait("g", "s", s_bank[n])
                sem = "sc%d_%d" % (me, i)
                send(transfer(high, helpers, sem, scores(me, i), scores(me, i)),
                     transfer(low, [cores[q] for q in same], sem, scores(me, i), scores(me, i)))

    wait("t", "v", k_lc)
    t_o = t(E.matmul(T.b7[:, 0:16], T.LC[:], T.DT[:], True, True))
    wait("t", "ldq", 16)
    t_q = t(E.matmul(T.b0[:, 0:256], T.G8[0:8, :], T.Q8[0:8, :], True, True))
    wait("v", "t", t_o)
    v(V.tensor_copy(T.O16[:], T.b7[:, 0:16]))
    wait("v", "t", t_q)
    k = ts(T.FP[:, 0:256], T.b0[:, 0:256], T.PC4[:, 0:1], None, A.is_equal)
    wait("v", "v", k)
    wait("v", "s", cnt["s"])
    for i in range(len(BATCH)):
        for r in same + cross:
            wait("v", "sc%d_%d" % (r, i), eng)
    k = v(V.tensor_tensor(T.FP[:, 256:512], T.SW[:, 0:3136].indirect(T.O16[:]), T.FP[:, 0:256], A.mult))
    wait("t", "v", k)
    k = t(E.matmul(T.b1[0:8, 0:256], T.BDC[:], T.FP[:, 256:512], True, True))
    wait("v", "t", k)
    k = v(V.tensor_copy(T.AF[0:8, 0:48], T.b1[0:8, 0:48])) if False else v(V.tensor_copy(T.FP[0:8, 0:256], T.b1[0:8, 0:256]))
    wait("y", "v", k)
    SY.dma_start(T.y[:], T.FP[0:8, 0:256]).then_inc(T.sem.yo, 16)
    wait("y", "yo", 16)
    for name in ("v", "t", "s", "gi"):
        wait("g", name, cnt[name])
    wait("g", "snt", sent[0])
